import numpy as np
import ml_dtypes


def mxq(x, axis, fmt="e4m3"):
    dtype, down = {"e4m3": (ml_dtypes.float8_e4m3fn, 7), "e5m2": (ml_dtypes.float8_e5m2, 14)}[fmt]
    v = np.moveaxis(np.asarray(x, np.float32).astype(ml_dtypes.bfloat16).astype(np.float64), axis, -1)
    blocks = v.reshape(v.shape[:-1] + (-1, 32))
    amax = np.abs(blocks).max(-1, keepdims=True)
    byte = np.maximum(np.where(amax > 0, np.frexp(amax)[1] - 1 + 127, 0) - down, 1)
    scale = np.exp2(byte - 127.0)
    codes = (blocks / scale).astype(np.float32).astype(dtype).astype(np.float64)
    return np.moveaxis((codes * scale).reshape(v.shape), -1, axis)


WIDE = False


def mx_kscale(k):
    if not WIDE:
        return np.ones(k)
    levels = np.array([10, -10, 5, -5, 0])
    if k % 512:
        return np.exp2(np.random.permutation(np.resize(levels, k // 32))).repeat(32)
    a = np.empty((k // 512, 16))
    for p in range(k // 512):
        a[p, :8] = np.random.permutation(np.resize(levels, 8))
        for g in range(8):
            far = levels[np.abs(levels - a[p, g]) >= 10]
            a[p, g + 8] = far[np.random.randint(len(far))]
    return np.exp2(a.ravel()).repeat(32)


def f64(x):
    return np.asarray(x).astype(np.float64)


def striped(idx):
    return np.tile(idx.reshape(-1, 16).T, (8, 1)).astype(np.uint16)


def unstriped(offs):
    return offs[:16].T.reshape(-1).astype(np.int64)


E2M1 = np.array([0.0, 0.5, 1.0, 1.5, 2.0, 3.0, 4.0, 6.0, -0.0, -0.5, -1.0, -1.5, -2.0, -3.0, -4.0, -6.0])


def pack_weight(w, fmt):
    k, n = w.shape
    w = f64(np.asarray(w, np.float32).astype(ml_dtypes.bfloat16)).reshape(k // 32, 32, n)
    amax = np.abs(w).max(1)
    if fmt == "e4m3":
        byte = np.frexp(amax)[1] - 1 + 127 - 7
    else:
        mant, ex = np.frexp(amax / 6.0)
        byte = np.where(mant > 0.5, ex, ex - 1) + 127
    byte = np.clip(np.where(amax > 0, byte, 1), 1, 254)
    scaled = (w * np.exp2(127.0 - byte)[:, None, :]).reshape(k, n).astype(np.float32)
    by_word = np.ascontiguousarray(scaled.reshape(k // 512, 128, 4, n).transpose(0, 1, 3, 2))
    if fmt == "e4m3":
        words = by_word.astype(ml_dtypes.float8_e4m3fn).view(np.uint8)
    else:
        c = by_word.astype(ml_dtypes.float4_e2m1fn).view(np.uint8) & 0xF
        words = (c[..., 0::2] | (c[..., 1::2] << 4)).reshape(k // 512, 128, 2 * n)
    return np.ascontiguousarray(words), np.ascontiguousarray(byte.astype(np.uint8).reshape(k // 512, 16, n))


def unpack_weight(words, scales, fmt):
    g, _, n = scales.shape
    words = np.ascontiguousarray(words).reshape(g, 128, n, -1)
    if fmt == "e4m3":
        vals = words.view(ml_dtypes.float8_e4m3fn).astype(np.float64)
    else:
        nib = np.empty((g, 128, n, 4), np.uint8)
        nib[..., 0::2] = words & 0xF
        nib[..., 1::2] = words >> 4
        vals = E2M1[nib]
    vals = vals * np.repeat(np.exp2(scales.astype(np.float64) - 127.0), 8, axis=1)[..., None]
    return vals.transpose(0, 1, 3, 2).reshape(g * 512, n)


def gelu(v):
    return 0.5 * v * (1.0 + np.tanh(np.sqrt(2.0 / np.pi) * (v + 0.044715 * v**3)))


K, M, H, T, S, T2, S2, T3, P = 1024, 1024, 1024, 2048, 512, 1024, 512, 2048, 512

def setup_inputs():
    n = np.random.standard_normal
    s = mx_kscale(K)[:, None]
    u1 = mx_kscale(M)[:, None]
    u = mx_kscale(H)[:, None]
    tab_words, tab_scales = pack_weight(n((K, T)) * s, "e4m3")
    tab2_words, tab2_scales = pack_weight(n((H, T3)) / np.sqrt(H) / u, "e4m3")
    w2_words, w2_scales = pack_weight(n((M, H)) * 1.4 / np.sqrt(M) / u1 * u.T, "e2m1")
    return {
        "tab_words": tab_words, "tab_scales": tab_scales,
        "offs": striped(np.random.permutation(T)[:S]),
        "w1": (n((K, M)) * 1.6 / np.sqrt(K) / s).astype(np.float32),
        "gain": (np.exp(0.3 * n(M)) * u1[:, 0]).astype(np.float32),
        "w2_words": w2_words, "w2_scales": w2_scales,
        "page0": (n((H, T2)) * u).astype(np.float32),
        "wgs": np.exp(0.3 * n((128, S))).astype(np.float32),
        "offs3": striped(np.random.permutation(T2)[:S]),
        "tab2_words": tab2_words, "tab2_scales": tab2_scales,
        "offs2": striped(np.random.permutation(T3)[:S2]),
        "pos1": striped(np.random.permutation(T2)[:P]),
        "pos2": striped(np.random.permutation(T2)[:P]),
        "terr": (0.8 * n(S2)).astype(np.float32),
    }

def reference(tab_words, tab_scales, offs, w1, gain, w2_words, w2_scales, page0, wgs, offs3, tab2_words, tab2_scales, offs2, pos1, pos2, terr):
    v = unpack_weight(tab_words, tab_scales, "e4m3")[:, unstriped(offs)]
    v2 = unpack_weight(tab2_words, tab2_scales, "e4m3")[:, unstriped(offs2)]
    w2 = unpack_weight(w2_words, w2_scales, "e2m1")
    x = f64(gain)[:, None] * np.tanh(mxq(f64(w1), 0, "e4m3").T @ v)
    h = w2.T @ mxq(x, 0, "e4m3")
    page = f64(page0).copy()
    page[:, unstriped(offs3)] = np.tile(f64(wgs), (H // 128, 1)) * h
    e = v2.T @ mxq(page, 0, "e4m3")
    core = e[:, unstriped(pos1)]
    rim = e[:, unstriped(pos2)]
    return np.maximum(core, rim + f64(terr)[:, None])

@@ -1,0 +1,314 @@
+from contextlib import ExitStack
+
+import concourse.mybir as mybir
+
+K, M, H, T, S, T2, S2, T3, NPAIR = 1024, 1024, 1024, 2048, 512, 1024, 512, 2048, 512
+FLOPS = 2 * K * M * S + 2 * M * H * S + 2 * H * S2 * T2
+
+F32 = mybir.dt.float32
+BF16 = mybir.dt.bfloat16
+I32 = mybir.dt.int32
+U32 = mybir.dt.uint32
+U16 = mybir.dt.uint16
+U8 = mybir.dt.uint8
+FP8X4 = mybir.dt.float8_e4m3fn_x4
+FP4X4 = mybir.dt.float4_e2m1fn_x4
+ALU = mybir.AluOpType
+TANH = mybir.ActivationFunctionType.Tanh
+
+P = 128
+PACK = 4
+KP = P * PACK
+PASSES = 2
+QUADS = 4
+JQ = 128
+
+
+def tile_list_zircon_peak_scores_kernel(
+    tc, tab_words, tab_scales, offs, w1, gain, w2_words, w2_scales, page0, wgs, offs3,
+    tab2_words, tab2_scales, offs2, pos1, pos2, terr, out,
+):
+    nc = tc.nc
+    with ExitStack() as ctx:
+        lists = ctx.enter_context(tc.tile_pool(name="lists", bufs=1))
+        sb = ctx.enter_context(tc.tile_pool(name="sb", bufs=1))
+        psum = ctx.enter_context(tc.psum_pool(name="psum", bufs=1))
+
+        def new(shape, dtype, name, tag=None):
+            return sb.tile(shape, dtype, name=name, tag=tag or name, align_bytes=64)
+
+        def bank(shape, name, n):
+            return psum.tile(shape, F32, name=name, tag="bank%d" % n)
+
+        def load_list(src, name):
+            tile = lists.tile([P, S // 16], U16, name=name)
+            nc.sync.dma_start(tile[:], src)
+            return tile
+
+        def load_words(src, a, name):
+            tile = new([P, T], I32, name)
+            nc.sync.dma_start(out=tile[:], in_=src[a].rearrange("p t i -> p (t i)").bitcast(I32))
+            return tile
+
+        def load_table_scales(tile, src):
+            for quad in range(QUADS):
+                nc.sync.dma_start(
+                    out=tile[32 * quad : 32 * quad + 4 * PASSES, :].bitcast(I32),
+                    in_=src[:, 4 * quad : 4 * quad + 4, :].bitcast(I32),
+                )
+
+        def load_w1(b, a, pieces):
+            rows = w1[a * KP : (a + 1) * KP, b * KP : (b + 1) * KP].rearrange("(p i) n -> p i n", i=PACK)
+            width = KP // pieces
+            tiles = []
+            for c in range(pieces):
+                tile = new([P, PACK, width], F32, "w1raw%d%d%d" % (b, a, c))
+                nc.sync.dma_start(out=tile[:], in_=rows[:, :, c * width : (c + 1) * width])
+                tiles.append(tile)
+            return tiles
+
+        def load_page(b, t):
+            tile = new([P, T2], F32, "page%d%d" % (b, t))
+            nc.sync.dma_start(out=tile[:], in_=page0.rearrange("(b p t) j -> b t p j", p=P, t=PACK)[b, t])
+            return tile
+
+        def load_wgs(half):
+            tile = new([P, 2, S], F32, "wgs%d" % half)
+            rows = wgs.rearrange("(q t) j -> q t j", t=PACK)[:, 2 * half : 2 * half + 2, :]
+            for quad in range(QUADS):
+                nc.sync.dma_start(out=tile[32 * quad : 32 * quad + 32, :, :], in_=rows)
+            return tile
+
+        def gather(dst, window, offsets):
+            nc.vector.tensor_copy(dst, window.indirect(offsets))
+
+        tab_sc = new([P, T], U8, "tab_sc")
+        w2_sc_raw = new([P, PASSES, H], U8, "w2_sc_raw")
+        tab2_sc = new([P, T3], U8, "tab2_sc")
+        nc.vector.memset(tab_sc[:].bitcast(I32), 0)
+        nc.vector.memset(w2_sc_raw[:].rearrange("p a c -> p (a c)").bitcast(I32), 0)
+        nc.vector.memset(tab2_sc[:].bitcast(I32), 0)
+
+        w1_raw = {}
+        w1_raw[0, 0] = load_w1(0, 0, 1)
+        load_table_scales(tab_sc, tab_scales)
+        w1_raw[0, 1] = load_w1(0, 1, 1)
+        offs_sb = load_list(offs, "offs_sb")
+        tab_w = [load_words(tab_words, 0, "tab_w0")]
+        w2_raw = new([P, PASSES, H], U16, "w2_raw")
+        nc.sync.dma_start(out=w2_raw[:].bitcast(I32), in_=w2_words.rearrange("a p c -> p a c").bitcast(I32))
+        for quad in range(QUADS):
+            nc.sync.dma_start(
+                out=w2_sc_raw[32 * quad : 32 * quad + 4, :, :].bitcast(I32),
+                in_=w2_scales[:, 4 * quad : 4 * quad + 4, :].rearrange("a r c -> r a c").bitcast(I32),
+            )
+        tab_w.append(load_words(tab_words, 1, "tab_w1"))
+        load_table_scales(tab2_sc, tab2_scales)
+        w1_raw[1, 0] = load_w1(1, 0, 1)
+        gain_sb = new([P, PASSES, PACK], F32, "gain_sb")
+        nc.sync.dma_start(out=gain_sb[:], in_=gain.rearrange("(b p t) -> p b t", p=P, t=PACK))
+        offs2_sb = load_list(offs2, "offs2_sb")
+        w1_raw[1, 1] = load_w1(1, 1, 2)
+        offs3_sb = load_list(offs3, "offs3_sb")
+        page = {}
+        page[0, 0] = load_page(0, 0)
+        wgs_sb = [load_wgs(0)]
+        tab2_w = [load_words(tab2_words, 0, "tab2_w0")]
+        page[0, 1] = load_page(0, 1)
+        wgs_sb.append(load_wgs(1))
+        page[0, 2] = load_page(0, 2)
+        page[1, 2] = load_page(1, 2)
+        page[0, 3] = load_page(0, 3)
+        tab2_w.append(load_words(tab2_words, 1, "tab2_w1"))
+        for t in (0, 1, 3):
+            page[1, t] = load_page(1, t)
+        pos1_sb = load_list(pos1, "pos1_sb")
+        pos2_sb = load_list(pos2, "pos2_sb")
+        terr_sb = new([P, S2 // P], F32, "terr_sb")
+        with nc.allow_non_contiguous_dma(reason="one offset a partition"):
+            nc.sync.dma_start(out=terr_sb[:], in_=terr.rearrange("(u p) -> p u", p=P))
+
+        w1_codes, w1_sc = {}, {}
+
+        def weave_w1(engine_copy, dst, raw, q0, q1, base):
+            engine_copy(
+                out=dst[:, :, q0:q1, :].rearrange("p t q i -> p q i t"),
+                in_=raw[:, :, PACK * (q0 - base) : PACK * (q1 - base)].rearrange("p i (q t) -> p q i t", t=PACK),
+            )
+
+        def quantize_w1(b, a, woven):
+            w1_codes[b, a] = new([P, KP], U32, "w1c%d%d" % (b, a))
+            w1_sc[b, a] = new([P, KP], U8, "w1s%d%d" % (b, a))
+            nc.vector.quantize_mx(
+                out=w1_codes[b, a][:].bitcast(FP8X4), scales=w1_sc[b, a][:],
+                in_=woven[:].rearrange("p t q i -> p (t q i)"),
+            )
+
+        woven = {}
+        for a in range(PASSES):
+            woven[0, a] = new([P, PACK, P, PACK], BF16, "w1bf0%d" % a, tag="w1bf%d" % a)
+        weave_w1(nc.scalar.copy, woven[0, 0], w1_raw[0, 0][0], 0, P, 0)
+        weave_w1(nc.scalar.copy, woven[0, 1], w1_raw[0, 1][0], 0, P, 0)
+
+        v_sc = new([P, S], U8, "v_sc")
+        gather(v_sc[:], tab_sc[:], offs_sb[:])
+        quantize_w1(0, 0, woven[0, 0])
+        v = []
+        for a in range(PASSES):
+            v.append(new([P, S], U32, "v%d" % a))
+            gather(v[a][:], tab_w[a][:].bitcast(U32), offs_sb[:])
+        quantize_w1(0, 1, woven[0, 1])
+
+        for a in range(PASSES):
+            woven[1, a] = new([P, PACK, P, PACK], BF16, "w1bf1%d" % a, tag="w1bf%d" % a)
+        weave_w1(nc.vector.tensor_copy, woven[1, 0], w1_raw[1, 0][0], 0, P, 0)
+        quantize_w1(1, 0, woven[1, 0])
+        weave_w1(nc.scalar.copy, woven[1, 1], w1_raw[1, 1][0], 0, 64, 0)
+        weave_w1(nc.vector.tensor_copy, woven[1, 1], w1_raw[1, 1][1], 64, P, 64)
+        quantize_w1(1, 1, woven[1, 1])
+
+        w2_c = new([P, PASSES, H], U16, "w2_c")
+        nc.vector.tensor_copy(
+            out=w2_c[:].rearrange("p a (b t q) -> p (a b) t q", t=PACK, q=P),
+            in_=w2_raw[:].rearrange("p a (b q t) -> p (a b) t q", t=PACK, q=P),
+        )
+        w2_sc = new([P, PASSES, H], U8, "w2_sc")
+        nc.vector.tensor_copy(
+            out=w2_sc[:].rearrange("p a (b t q) -> p (a b) t q", t=PACK, q=P),
+            in_=w2_sc_raw[:].rearrange("p a (b q t) -> p (a b) t q", t=PACK, q=P),
+        )
+        v2_sc = new([P, S2], U8, "v2_sc")
+        gather(v2_sc[:], tab2_sc[:], offs2_sb[:])
+
+        x_codes, x_sc = [], []
+        for b in range(PASSES):
+            acc = [bank([P, PACK, JQ], "acc1_%d%d" % (b, jq), 4 * b + jq) for jq in range(S // JQ)]
+            for a in range(PASSES):
+                for jq in range(S // JQ):
+                    cols = slice(jq * JQ, (jq + 1) * JQ)
+                    for t in range(PACK):
+                        nc.tensor.matmul_mx(
+                            out=acc[jq][:, t, :],
+                            lhsT=w1_codes[b, a][:, t * P : (t + 1) * P].bitcast(FP8X4),
+                            lhsT_scale=w1_sc[b, a][:, t * P : (t + 1) * P],
+                            rhs=v[a][:, cols].bitcast(FP8X4),
+                            rhs_scale=v_sc[4 * a : P, cols],
+                            start=(a == 0 and t == 0),
+                            stop=(a == PASSES - 1 and t == PACK - 1),
+                        )
+            x_bf = new([P, S, PACK], BF16, "x_bf%d" % b, tag="w1bf%d" % (1 - b))
+            x_codes.append(new([P, S], U32, "x_c%d" % b))
+            x_sc.append(new([P, S], U8, "x_s%d" % b))
+            for jq in range(S // JQ):
+                th = new([P, JQ, PACK], F32, "th%d%d" % (b, jq))
+                nc.scalar.activation(out=th[:], in_=acc[jq][:].rearrange("p t j -> p j t"), func=TANH)
+                nc.vector.tensor_tensor(
+                    out=x_bf[:, jq * JQ : (jq + 1) * JQ, :], in0=th[:],
+                    in1=gain_sb[:, b : b + 1, :].to_broadcast([P, JQ, PACK]), op=ALU.mult,
+                )
+            for half in range(2):
+                cols = slice(half * S // 2, (half + 1) * S // 2)
+                nc.vector.quantize_mx(
+                    out=x_codes[b][:, cols].bitcast(FP8X4), scales=x_sc[b][:, cols],
+                    in_=x_bf[:, cols, :].rearrange("p j t -> p (j t)"),
+                )
+
+        h = {}
+        order = [(0, 0), (0, 1), (0, 2), (1, 2), (0, 3), (1, 0), (1, 1), (1, 3)]
+        for n, (b, t) in enumerate(order):
+            if True:
+                u = PACK * b + t
+                acc2 = bank([P, S], "acc2_%d" % u, n)
+                for a in range(PASSES):
+                    cols = slice(u * P, (u + 1) * P)
+                    nc.tensor.matmul_mx(
+                        out=acc2[:],
+                        lhsT=w2_c[:, a, cols].bitcast(FP4X4),
+                        lhsT_scale=w2_sc[:, a, cols],
+                        rhs=x_codes[a][:].bitcast(FP8X4),
+                        rhs_scale=x_sc[a][:],
+                        start=(a == 0),
+                        stop=(a == PASSES - 1),
+                    )
+                h[b, t] = new([P, S], F32, "h%d" % u)
+                nc.scalar.copy(out=h[b, t][:], in_=acc2[:])
+
+        page_bf = [new([P, T2, PACK], BF16, "page_bf%d" % b) for b in range(PASSES)]
+        page_sc = [new([P, T2], U8, "page_s%d" % b) for b in range(PASSES)]
+        order = [(0, 0), (0, 1), (0, 2), (1, 2), (0, 3), (1, 0), (1, 1), (1, 3)]
+        v2, page_c = {}, []
+        v2[0, 0] = new([P, S2], U32, "v2_0")
+        v2[0, 1] = v2[0, 0][:, S2 // 2 : S2]
+        gather(v2[0, 0][:], tab2_w[0][:].bitcast(U32), offs2_sb[:])
+        for n, (b, t) in enumerate(order):
+            nc.vector.tensor_tensor(
+                page[b, t][:].indirect(offs3_sb[:]), h[b, t][:], wgs_sb[t // 2][:, t % 2, :], ALU.mult
+            )
+            if n < len(order) - 1:
+                nc.scalar.copy(out=page_bf[b][:, :, t], in_=page[b, t][:])
+            if n == 3:
+                v2[1, 0] = new([P, S2 // 2], U32, "v2_10")
+                gather(v2[1, 0][:], tab2_w[1][:].bitcast(U32), offs2_sb[:, 0:16])
+            if n == len(order) - 2:
+                page_c.append(new([P, T2], U32, "page_c0", tag="h%d" % (PACK * b + t)))
+                nc.vector.quantize_mx(
+                    out=page_c[0][:].bitcast(FP8X4), scales=page_sc[0][:],
+                    in_=page_bf[0][:].rearrange("p j t -> p (j t)"),
+                )
+        last = page[PASSES - 1, PACK - 1]
+        nc.vector.tensor_copy(out=page_bf[1][:, 0:512, PACK - 1], in_=last[:, 0:512])
+        nc.vector.tensor_copy(out=page_bf[1][:, 512:640, PACK - 1], in_=last[:, 512:640])
+        nc.scalar.copy(out=page_bf[1][:, 640:T2, PACK - 1], in_=last[:, 640:T2])
+        page_c.append(new([P, T2], U32, "page_c1"))
+        for half in range(2):
+            cols = slice(half * 512, (half + 1) * 512)
+            nc.vector.quantize_mx(
+                out=page_c[1][:, cols].bitcast(FP8X4), scales=page_sc[1][:, cols],
+                in_=page_bf[1][:, cols, :].rearrange("p j t -> p (j t)"),
+            )
+        v2[1, 1] = new([P, S2 // 2], U32, "v2_11", tag="page_bf1")
+        gather(v2[1, 1][:], tab2_w[1][:].bitcast(U32), offs2_sb[:, 16:32])
+
+        tiles = S2 // P
+        acc3 = [[bank([P, 512], "acc3_%d%d" % (u, half), 2 * u + half) for half in range(2)] for u in range(tiles)]
+        for a in range(PASSES):
+            for u in range(tiles):
+                for half in range(2):
+                    cols = slice(half * 512, (half + 1) * 512)
+                    nc.tensor.matmul_mx(
+                        out=acc3[u][half][:],
+                        lhsT=v2[a, u // 2][:, (u % 2) * P : (u % 2 + 1) * P].bitcast(FP8X4),
+                        lhsT_scale=v2_sc[4 * a : P, u * P : (u + 1) * P],
+                        rhs=page_c[a][:, cols].bitcast(FP8X4),
+                        rhs_scale=page_sc[a][:, cols],
+                        start=(a == 0),
+                        stop=(a == PASSES - 1),
+                    )
+        e = []
+        for u in range(tiles):
+            e.append(new([P, T2], F32, "e%d" % u, tag="w1raw%d%d0" % (u // 2, u % 2)))
+            for half in range(2):
+                copy = nc.vector.tensor_copy if (u, half) == (0, 1) else nc.scalar.copy
+                copy(out=e[u][:, half * 512 : (half + 1) * 512], in_=acc3[u][half][:])
+
+        steps = [(u, 0, NPAIR) for u in range(tiles - 1)] + [(tiles - 1, 0, NPAIR // 2), (tiles - 1, NPAIR // 2, NPAIR)]
+        picked = []
+
+        def finish(n):
+            u, j0, j1 = steps[n]
+            core, rim = picked[n]
+            res = new([P, j1 - j0], F32, "res%d" % n, tag="th0%d" % (n % 4))
+            nc.vector.scalar_tensor_tensor(
+                out=res[:], in0=rim[:], scalar=terr_sb[:, u : u + 1], in1=core[:], op0=ALU.add, op1=ALU.max
+            )
+            nc.sync.dma_start(out=out[u * P : (u + 1) * P, j0:j1], in_=res[:])
+
+        for n, (u, j0, j1) in enumerate(steps):
+            core = new([P, j1 - j0], F32, "core%d" % n, tag="th1%d" % (n % 4))
+            rim = new([P, j1 - j0], F32, "rim%d" % n, tag="h%d" % n)
+            picked.append((core, rim))
+            gather(core[:], e[u][:], pos1_sb[:, j0 // 16 : j1 // 16])
+            if n > 0:
+                finish(n - 1)
+            gather(rim[:], e[u][:], pos2_sb[:, j0 // 16 : j1 // 16])
+        finish(len(steps) - 1)

@@ -20,8 +20,13 @@ P = 128
 PACK = 4
 KP = P * PACK
 PASSES = 2
-QUADS = 4
-JQ = 128
+BANK = 512
+JQ = BANK // PACK
+PER_COLUMN = 16
+QUADRANT = 32
+QUADRANT_ORDER = (0, 2, 1, 3)
+VECTOR_COLUMNS = 640
+PAGE_ORDER = ((0, 0), (0, 1), (0, 2), (1, 2), (0, 3), (1, 0), (1, 1), (1, 3))
 
 
 def tile_list_zircon_peak_scores_kernel(
@@ -37,11 +42,11 @@ def tile_list_zircon_peak_scores_kernel(
         def new(shape, dtype, name, tag=None):
             return sb.tile(shape, dtype, name=name, tag=tag or name, align_bytes=64)
 
-        def bank(shape, name, n):
-            return psum.tile(shape, F32, name=name, tag="bank%d" % n)
+        def bank(shape, name, number):
+            return psum.tile(shape, F32, name=name, tag="bank%d" % number)
 
         def load_list(src, name):
-            tile = lists.tile([P, S // 16], U16, name=name)
+            tile = lists.tile([P, S // PER_COLUMN], U16, name=name)
             nc.sync.dma_start(tile[:], src)
             return tile
 
@@ -50,10 +55,17 @@ def tile_list_zircon_peak_scores_kernel(
             nc.sync.dma_start(out=tile[:], in_=src[a].rearrange("p t i -> p (t i)").bitcast(I32))
             return tile
 
+        def load_w2_scales(tile):
+            for quad in QUADRANT_ORDER:
+                nc.scalar.dma_start(
+                    out=tile[QUADRANT * quad : QUADRANT * quad + 4, :, :].bitcast(I32),
+                    in_=w2_scales[:, 4 * quad : 4 * quad + 4, :].rearrange("a r c -> r a c").bitcast(I32),
+                )
+
         def load_table_scales(tile, src):
-            for quad in range(QUADS):
-                nc.sync.dma_start(
-                    out=tile[32 * quad : 32 * quad + 4 * PASSES, :].bitcast(I32),
+            for quad in QUADRANT_ORDER:
+                nc.gpsimd.dma_start(
+                    out=tile[QUADRANT * quad : QUADRANT * quad + 4 * PASSES, :].bitcast(I32),
                     in_=src[:, 4 * quad : 4 * quad + 4, :].bitcast(I32),
                 )
 
@@ -72,12 +84,12 @@ def tile_list_zircon_peak_scores_kernel(
             nc.sync.dma_start(out=tile[:], in_=page0.rearrange("(b p t) j -> b t p j", p=P, t=PACK)[b, t])
             return tile
 
-        def load_wgs(half):
-            tile = new([P, 2, S], F32, "wgs%d" % half)
-            rows = wgs.rearrange("(q t) j -> q t j", t=PACK)[:, 2 * half : 2 * half + 2, :]
-            for quad in range(QUADS):
-                nc.sync.dma_start(out=tile[32 * quad : 32 * quad + 32, :, :], in_=rows)
-            return tile
+        def load_wgs(t0, t1):
+            tile = new([P, t1 - t0, S], F32, "wgs%d" % t0)
+            rows = wgs.rearrange("(q t) j -> q t j", t=PACK)[:, t0:t1, :]
+            for quad in QUADRANT_ORDER:
+                nc.sync.dma_start(out=tile[QUADRANT * quad : QUADRANT * (quad + 1), :, :], in_=rows)
+            return [tile[:, t - t0, :] for t in range(t0, t1)]
 
         def gather(dst, window, offsets):
             nc.vector.tensor_copy(dst, window.indirect(offsets))
@@ -85,38 +97,34 @@ def tile_list_zircon_peak_scores_kernel(
         tab_sc = new([P, T], U8, "tab_sc")
         w2_sc_raw = new([P, PASSES, H], U8, "w2_sc_raw")
         tab2_sc = new([P, T3], U8, "tab2_sc")
-        nc.vector.memset(tab_sc[:].bitcast(I32), 0)
         nc.vector.memset(w2_sc_raw[:].rearrange("p a c -> p (a c)").bitcast(I32), 0)
+        nc.vector.memset(tab_sc[:].bitcast(I32), 0)
         nc.vector.memset(tab2_sc[:].bitcast(I32), 0)
 
-        w1_raw = {}
-        w1_raw[0, 0] = load_w1(0, 0, 1)
+        load_w2_scales(w2_sc_raw)
         load_table_scales(tab_sc, tab_scales)
-        w1_raw[0, 1] = load_w1(0, 1, 1)
+        load_table_scales(tab2_sc, tab2_scales)
         offs_sb = load_list(offs, "offs_sb")
-        tab_w = [load_words(tab_words, 0, "tab_w0")]
+        offs2_sb = load_list(offs2, "offs2_sb")
         w2_raw = new([P, PASSES, H], U16, "w2_raw")
         nc.sync.dma_start(out=w2_raw[:].bitcast(I32), in_=w2_words.rearrange("a p c -> p a c").bitcast(I32))
-        for quad in range(QUADS):
-            nc.sync.dma_start(
-                out=w2_sc_raw[32 * quad : 32 * quad + 4, :, :].bitcast(I32),
-                in_=w2_scales[:, 4 * quad : 4 * quad + 4, :].rearrange("a r c -> r a c").bitcast(I32),
-            )
-        tab_w.append(load_words(tab_words, 1, "tab_w1"))
-        load_table_scales(tab2_sc, tab2_scales)
-        w1_raw[1, 0] = load_w1(1, 0, 1)
+        w1_raw = {}
+        w1_raw[0, 0] = load_w1(0, 0, 1)
+        w1_raw[0, 1] = load_w1(0, 1, 1)
+        tab_w = [load_words(tab_words, a, "tab_w%d" % a) for a in range(PASSES)]
         gain_sb = new([P, PASSES, PACK], F32, "gain_sb")
         nc.sync.dma_start(out=gain_sb[:], in_=gain.rearrange("(b p t) -> p b t", p=P, t=PACK))
-        offs2_sb = load_list(offs2, "offs2_sb")
+        w1_raw[1, 0] = load_w1(1, 0, 1)
         w1_raw[1, 1] = load_w1(1, 1, 2)
         offs3_sb = load_list(offs3, "offs3_sb")
         page = {}
         page[0, 0] = load_page(0, 0)
-        wgs_sb = [load_wgs(0)]
+        wgs_sb = load_wgs(0, 1)
         tab2_w = [load_words(tab2_words, 0, "tab2_w0")]
         page[0, 1] = load_page(0, 1)
-        wgs_sb.append(load_wgs(1))
+        wgs_sb.extend(load_wgs(1, 2))
         page[0, 2] = load_page(0, 2)
+        wgs_sb.extend(load_wgs(2, PACK))
         page[1, 2] = load_page(1, 2)
         page[0, 3] = load_page(0, 3)
         tab2_w.append(load_words(tab2_words, 1, "tab2_w1"))
@@ -125,51 +133,34 @@ def tile_list_zircon_peak_scores_kernel(
         pos1_sb = load_list(pos1, "pos1_sb")
         pos2_sb = load_list(pos2, "pos2_sb")
         terr_sb = new([P, S2 // P], F32, "terr_sb")
-        with nc.allow_non_contiguous_dma(reason="one offset a partition"):
+        with nc.allow_non_contiguous_dma(reason="terr[128 u + p] goes to partition p, column u"):
             nc.sync.dma_start(out=terr_sb[:], in_=terr.rearrange("(u p) -> p u", p=P))
 
         w1_codes, w1_sc = {}, {}
 
-        def weave_w1(engine_copy, dst, raw, q0, q1, base):
+        def weave_w1(engine_copy, dst, raw, q0, q1):
             engine_copy(
                 out=dst[:, :, q0:q1, :].rearrange("p t q i -> p q i t"),
-                in_=raw[:, :, PACK * (q0 - base) : PACK * (q1 - base)].rearrange("p i (q t) -> p q i t", t=PACK),
+                in_=raw[:].rearrange("p i (q t) -> p q i t", t=PACK),
             )
 
-        def quantize_w1(b, a, woven):
+        def quantize_w1(b, a, woven_tile):
             w1_codes[b, a] = new([P, KP], U32, "w1c%d%d" % (b, a))
             w1_sc[b, a] = new([P, KP], U8, "w1s%d%d" % (b, a))
             nc.vector.quantize_mx(
                 out=w1_codes[b, a][:].bitcast(FP8X4), scales=w1_sc[b, a][:],
-                in_=woven[:].rearrange("p t q i -> p (t q i)"),
+                in_=woven_tile[:].rearrange("p t q i -> p (t q i)"),
             )
 
-        woven = {}
+        w1_bf = {}
         for a in range(PASSES):
-            woven[0, a] = new([P, PACK, P, PACK], BF16, "w1bf0%d" % a, tag="w1bf%d" % a)
-        weave_w1(nc.scalar.copy, woven[0, 0], w1_raw[0, 0][0], 0, P, 0)
-        weave_w1(nc.scalar.copy, woven[0, 1], w1_raw[0, 1][0], 0, P, 0)
+            w1_bf[0, a] = new([P, PACK, P, PACK], BF16, "w1bf0%d" % a, tag="w1bf%d" % a)
+        weave_w1(nc.scalar.copy, w1_bf[0, 0], w1_raw[0, 0][0], 0, P)
+        weave_w1(nc.scalar.copy, w1_bf[0, 1], w1_raw[0, 1][0], 0, P)
 
-        v_sc = new([P, S], U8, "v_sc")
-        gather(v_sc[:], tab_sc[:], offs_sb[:])
-        quantize_w1(0, 0, woven[0, 0])
-        v = []
-        for a in range(PASSES):
-            v.append(new([P, S], U32, "v%d" % a))
-            gather(v[a][:], tab_w[a][:].bitcast(U32), offs_sb[:])
-        quantize_w1(0, 1, woven[0, 1])
-
-        for a in range(PASSES):
-            woven[1, a] = new([P, PACK, P, PACK], BF16, "w1bf1%d" % a, tag="w1bf%d" % a)
-        weave_w1(nc.vector.tensor_copy, woven[1, 0], w1_raw[1, 0][0], 0, P, 0)
-        quantize_w1(1, 0, woven[1, 0])
-        weave_w1(nc.scalar.copy, woven[1, 1], w1_raw[1, 1][0], 0, 64, 0)
-        weave_w1(nc.vector.tensor_copy, woven[1, 1], w1_raw[1, 1][1], 64, P, 64)
-        quantize_w1(1, 1, woven[1, 1])
-
-        w2_c = new([P, PASSES, H], U16, "w2_c")
+        w2_codes = new([P, PASSES, H], U16, "w2_c")
         nc.vector.tensor_copy(
-            out=w2_c[:].rearrange("p a (b t q) -> p (a b) t q", t=PACK, q=P),
+            out=w2_codes[:].rearrange("p a (b t q) -> p (a b) t q", t=PACK, q=P),
             in_=w2_raw[:].rearrange("p a (b q t) -> p (a b) t q", t=PACK, q=P),
         )
         w2_sc = new([P, PASSES, H], U8, "w2_sc")
@@ -177,27 +168,44 @@ def tile_list_zircon_peak_scores_kernel(
             out=w2_sc[:].rearrange("p a (b t q) -> p (a b) t q", t=PACK, q=P),
             in_=w2_sc_raw[:].rearrange("p a (b q t) -> p (a b) t q", t=PACK, q=P),
         )
-        v2_sc = new([P, S2], U8, "v2_sc")
+        v_sc = new([P, S], U8, "v_sc")
+        gather(v_sc[:], tab_sc[:], offs_sb[:])
+        quantize_w1(0, 0, w1_bf[0, 0])
+        v_codes = []
+        for a in range(PASSES):
+            v_codes.append(new([P, S], U32, "v%d" % a))
+            gather(v_codes[a][:], tab_w[a][:].bitcast(U32), offs_sb[:])
+        quantize_w1(0, 1, w1_bf[0, 1])
+
+        for a in range(PASSES):
+            w1_bf[1, a] = new([P, PACK, P, PACK], BF16, "w1bf1%d" % a, tag="w1bf%d" % a)
+        weave_w1(nc.vector.tensor_copy, w1_bf[1, 0], w1_raw[1, 0][0], 0, P)
+        quantize_w1(1, 0, w1_bf[1, 0])
+        weave_w1(nc.scalar.copy, w1_bf[1, 1], w1_raw[1, 1][0], 0, P // 2)
+        weave_w1(nc.scalar.copy, w1_bf[1, 1], w1_raw[1, 1][1], P // 2, P)
+        quantize_w1(1, 1, w1_bf[1, 1])
+
+        v2_sc = new([P, S2], U8, "v2_sc", tag="tab_w1")
         gather(v2_sc[:], tab2_sc[:], offs2_sb[:])
 
         x_codes, x_sc = [], []
         for b in range(PASSES):
-            acc = [bank([P, PACK, JQ], "acc1_%d%d" % (b, jq), 4 * b + jq) for jq in range(S // JQ)]
-            for a in range(PASSES):
-                for jq in range(S // JQ):
+            acc = [bank([P, PACK, JQ], "acc1_%d%d" % (b, jq), PACK * b + jq) for jq in range(S // JQ)]
+            for jq in range(S // JQ):
+                for a in range(PASSES):
                     cols = slice(jq * JQ, (jq + 1) * JQ)
                     for t in range(PACK):
                         nc.tensor.matmul_mx(
                             out=acc[jq][:, t, :],
                             lhsT=w1_codes[b, a][:, t * P : (t + 1) * P].bitcast(FP8X4),
                             lhsT_scale=w1_sc[b, a][:, t * P : (t + 1) * P],
-                            rhs=v[a][:, cols].bitcast(FP8X4),
+                            rhs=v_codes[a][:, cols].bitcast(FP8X4),
                             rhs_scale=v_sc[4 * a : P, cols],
                             start=(a == 0 and t == 0),
                             stop=(a == PASSES - 1 and t == PACK - 1),
                         )
-            x_bf = new([P, S, PACK], BF16, "x_bf%d" % b, tag="w1bf%d" % (1 - b))
-            x_codes.append(new([P, S], U32, "x_c%d" % b))
+            x_bf = new([P, S, PACK], BF16, "x_bf%d" % b, tag=("w1bf0", "x_bf1")[b])
+            x_codes.append(new([P, S], U32, "x_c%d" % b, tag=("w1bf1", "x_c1")[b]))
             x_sc.append(new([P, S], U8, "x_s%d" % b))
             for jq in range(S // JQ):
                 th = new([P, JQ, PACK], F32, "th%d%d" % (b, jq))
@@ -213,73 +221,72 @@ def tile_list_zircon_peak_scores_kernel(
                     in_=x_bf[:, cols, :].rearrange("p j t -> p (j t)"),
                 )
 
+        v2_codes = {}
+        v2_codes[0, 0] = new([P, S2], U32, "v2_0", tag="x_bf1")
+        v2_codes[0, 1] = v2_codes[0, 0][:, S2 // 2 : S2]
+        gather(v2_codes[0, 0][:], tab2_w[0][:].bitcast(U32), offs2_sb[:])
+        half_list = S2 // 2 // PER_COLUMN
+
         h = {}
-        order = [(0, 0), (0, 1), (0, 2), (1, 2), (0, 3), (1, 0), (1, 1), (1, 3)]
-        for n, (b, t) in enumerate(order):
-            if True:
-                u = PACK * b + t
-                acc2 = bank([P, S], "acc2_%d" % u, n)
-                for a in range(PASSES):
-                    cols = slice(u * P, (u + 1) * P)
-                    nc.tensor.matmul_mx(
-                        out=acc2[:],
-                        lhsT=w2_c[:, a, cols].bitcast(FP4X4),
-                        lhsT_scale=w2_sc[:, a, cols],
-                        rhs=x_codes[a][:].bitcast(FP8X4),
-                        rhs_scale=x_sc[a][:],
-                        start=(a == 0),
-                        stop=(a == PASSES - 1),
-                    )
-                h[b, t] = new([P, S], F32, "h%d" % u)
-                nc.scalar.copy(out=h[b, t][:], in_=acc2[:])
+        for n, (b, t) in enumerate(PAGE_ORDER):
+            tile_number = PACK * b + t
+            cols = slice(tile_number * P, (tile_number + 1) * P)
+            acc2 = bank([P, S], "acc2_%d" % tile_number, n)
+            for a in range(PASSES):
+                nc.tensor.matmul_mx(
+                    out=acc2[:],
+                    lhsT=w2_codes[:, a, cols].bitcast(FP4X4),
+                    lhsT_scale=w2_sc[:, a, cols],
+                    rhs=x_codes[a][:].bitcast(FP8X4),
+                    rhs_scale=x_sc[a][:],
+                    start=(a == 0),
+                    stop=(a == PASSES - 1),
+                )
+            h[b, t] = new([P, S], F32, "h%d" % tile_number)
+            nc.scalar.copy(out=h[b, t][:], in_=acc2[:])
 
         page_bf = [new([P, T2, PACK], BF16, "page_bf%d" % b) for b in range(PASSES)]
         page_sc = [new([P, T2], U8, "page_s%d" % b) for b in range(PASSES)]
-        order = [(0, 0), (0, 1), (0, 2), (1, 2), (0, 3), (1, 0), (1, 1), (1, 3)]
-        v2, page_c = {}, []
-        v2[0, 0] = new([P, S2], U32, "v2_0")
-        v2[0, 1] = v2[0, 0][:, S2 // 2 : S2]
-        gather(v2[0, 0][:], tab2_w[0][:].bitcast(U32), offs2_sb[:])
-        for n, (b, t) in enumerate(order):
-            nc.vector.tensor_tensor(
-                page[b, t][:].indirect(offs3_sb[:]), h[b, t][:], wgs_sb[t // 2][:, t % 2, :], ALU.mult
-            )
-            if n < len(order) - 1:
+        page_codes = []
+        last = len(PAGE_ORDER) - 1
+        for n, (b, t) in enumerate(PAGE_ORDER):
+            nc.vector.tensor_tensor(page[b, t][:].indirect(offs3_sb[:]), h[b, t][:], wgs_sb[t], ALU.mult)
+            if n < last:
                 nc.scalar.copy(out=page_bf[b][:, :, t], in_=page[b, t][:])
-            if n == 3:
-                v2[1, 0] = new([P, S2 // 2], U32, "v2_10")
-                gather(v2[1, 0][:], tab2_w[1][:].bitcast(U32), offs2_sb[:, 0:16])
-            if n == len(order) - 2:
-                page_c.append(new([P, T2], U32, "page_c0", tag="h%d" % (PACK * b + t)))
+            if n == last // 2:
+                v2_codes[1, 0] = new([P, S2 // 2], U32, "v2_10")
+                gather(v2_codes[1, 0][:], tab2_w[1][:].bitcast(U32), offs2_sb[:, 0:half_list])
+            if n == last - 1:
+                page_codes.append(new([P, T2], U32, "page_c0", tag="h%d" % (PACK * b + t)))
                 nc.vector.quantize_mx(
-                    out=page_c[0][:].bitcast(FP8X4), scales=page_sc[0][:],
+                    out=page_codes[0][:].bitcast(FP8X4), scales=page_sc[0][:],
                     in_=page_bf[0][:].rearrange("p j t -> p (j t)"),
                 )
-        last = page[PASSES - 1, PACK - 1]
-        nc.vector.tensor_copy(out=page_bf[1][:, 0:512, PACK - 1], in_=last[:, 0:512])
-        nc.vector.tensor_copy(out=page_bf[1][:, 512:640, PACK - 1], in_=last[:, 512:640])
-        nc.scalar.copy(out=page_bf[1][:, 640:T2, PACK - 1], in_=last[:, 640:T2])
-        page_c.append(new([P, T2], U32, "page_c1"))
-        for half in range(2):
-            cols = slice(half * 512, (half + 1) * 512)
+        b, t = PAGE_ORDER[last]
+        nc.vector.tensor_copy(out=page_bf[b][:, 0:BANK, t], in_=page[b, t][:, 0:BANK])
+        nc.vector.tensor_copy(out=page_bf[b][:, BANK:VECTOR_COLUMNS, t], in_=page[b, t][:, BANK:VECTOR_COLUMNS])
+        nc.scalar.copy(out=page_bf[b][:, VECTOR_COLUMNS:T2, t], in_=page[b, t][:, VECTOR_COLUMNS:T2])
+        page_codes.append(new([P, T2], U32, "page_c1"))
+        for half in range(T2 // BANK):
+            cols = slice(half * BANK, (half + 1) * BANK)
             nc.vector.quantize_mx(
-                out=page_c[1][:, cols].bitcast(FP8X4), scales=page_sc[1][:, cols],
-                in_=page_bf[1][:, cols, :].rearrange("p j t -> p (j t)"),
+                out=page_codes[b][:, cols].bitcast(FP8X4), scales=page_sc[b][:, cols],
+                in_=page_bf[b][:, cols, :].rearrange("p j t -> p (j t)"),
             )
-        v2[1, 1] = new([P, S2 // 2], U32, "v2_11", tag="page_bf1")
-        gather(v2[1, 1][:], tab2_w[1][:].bitcast(U32), offs2_sb[:, 16:32])
+        v2_codes[1, 1] = new([P, S2 // 2], U32, "v2_11", tag="page_bf1")
+        gather(v2_codes[1, 1][:], tab2_w[1][:].bitcast(U32), offs2_sb[:, half_list : 2 * half_list])
 
         tiles = S2 // P
-        acc3 = [[bank([P, 512], "acc3_%d%d" % (u, half), 2 * u + half) for half in range(2)] for u in range(tiles)]
+        acc3 = [[bank([P, BANK], "acc3_%d%d" % (u, half), 2 * u + half) for half in range(2)] for u in range(tiles)]
         for a in range(PASSES):
             for u in range(tiles):
                 for half in range(2):
-                    cols = slice(half * 512, (half + 1) * 512)
+                    cols = slice(half * BANK, (half + 1) * BANK)
                     nc.tensor.matmul_mx(
                         out=acc3[u][half][:],
-                        lhsT=v2[a, u // 2][:, (u % 2) * P : (u % 2 + 1) * P].bitcast(FP8X4),
+                        lhsT=v2_codes[a, u // 2][:, (u % 2) * P : (u % 2 + 1) * P].bitcast(FP8X4),
                         lhsT_scale=v2_sc[4 * a : P, u * P : (u + 1) * P],
-                        rhs=page_c[a][:, cols].bitcast(FP8X4),
+                        rhs=page_codes[a][:, cols].bitcast(FP8X4),
                         rhs_scale=page_sc[a][:, cols],
                         start=(a == 0),
                         stop=(a == PASSES - 1),
@@ -289,7 +296,7 @@ def tile_list_zircon_peak_scores_kernel(
             e.append(new([P, T2], F32, "e%d" % u, tag="w1raw%d%d0" % (u // 2, u % 2)))
             for half in range(2):
                 copy = nc.vector.tensor_copy if (u, half) == (0, 1) else nc.scalar.copy
-                copy(out=e[u][:, half * 512 : (half + 1) * 512], in_=acc3[u][half][:])
+                copy(out=e[u][:, half * BANK : (half + 1) * BANK], in_=acc3[u][half][:])
 
         steps = [(u, 0, NPAIR) for u in range(tiles - 1)] + [(tiles - 1, 0, NPAIR // 2), (tiles - 1, NPAIR // 2, NPAIR)]
         picked = []
@@ -297,18 +304,19 @@ def tile_list_zircon_peak_scores_kernel(
         def finish(n):
             u, j0, j1 = steps[n]
             core, rim = picked[n]
-            res = new([P, j1 - j0], F32, "res%d" % n, tag="th0%d" % (n % 4))
+            res = new([P, j1 - j0], F32, "res%d" % n, tag="th0%d" % (n % PACK))
             nc.vector.scalar_tensor_tensor(
                 out=res[:], in0=rim[:], scalar=terr_sb[:, u : u + 1], in1=core[:], op0=ALU.add, op1=ALU.max
             )
             nc.sync.dma_start(out=out[u * P : (u + 1) * P, j0:j1], in_=res[:])
 
         for n, (u, j0, j1) in enumerate(steps):
-            core = new([P, j1 - j0], F32, "core%d" % n, tag="th1%d" % (n % 4))
+            entries = slice(j0 // PER_COLUMN, j1 // PER_COLUMN)
+            core = new([P, j1 - j0], F32, "core%d" % n, tag="th1%d" % (n % PACK))
             rim = new([P, j1 - j0], F32, "rim%d" % n, tag="h%d" % n)
             picked.append((core, rim))
-            gather(core[:], e[u][:], pos1_sb[:, j0 // 16 : j1 // 16])
+            gather(core[:], e[u][:], pos1_sb[:, entries])
             if n > 0:
                 finish(n - 1)
-            gather(rim[:], e[u][:], pos2_sb[:, j0 // 16 : j1 // 16])
+            gather(rim[:], e[u][:], pos2_sb[:, entries])
         finish(len(steps) - 1)

@@ -182,7 +182,7 @@ def tile_list_zircon_peak_scores_kernel(
         weave_w1(nc.vector.tensor_copy, w1_bf[1, 0], w1_raw[1, 0][0], 0, P)
         quantize_w1(1, 0, w1_bf[1, 0])
         weave_w1(nc.scalar.copy, w1_bf[1, 1], w1_raw[1, 1][0], 0, P // 2)
-        weave_w1(nc.scalar.copy, w1_bf[1, 1], w1_raw[1, 1][1], P // 2, P)
+        weave_w1(nc.vector.tensor_copy, w1_bf[1, 1], w1_raw[1, 1][1], P // 2, P)
         quantize_w1(1, 1, w1_bf[1, 1])
 
         v2_sc = new([P, S2], U8, "v2_sc", tag="tab_w1")

from contextlib import ExitStack

import concourse.mybir as mybir

K, M, H, T, S, T2, S2, T3, NPAIR = 1024, 1024, 1024, 2048, 512, 1024, 512, 2048, 512
FLOPS = 2 * K * M * S + 2 * M * H * S + 2 * H * S2 * T2

F32 = mybir.dt.float32
BF16 = mybir.dt.bfloat16
I32 = mybir.dt.int32
U32 = mybir.dt.uint32
U16 = mybir.dt.uint16
U8 = mybir.dt.uint8
FP8X4 = mybir.dt.float8_e4m3fn_x4
FP4X4 = mybir.dt.float4_e2m1fn_x4
ALU = mybir.AluOpType
TANH = mybir.ActivationFunctionType.Tanh

P = 128
PACK = 4
KP = P * PACK
PASSES = 2
BANK = 512
JQ = BANK // PACK
PER_COLUMN = 16
QUADRANT = 32
QUADRANT_ORDER = (0, 2, 1, 3)
VECTOR_COLUMNS = 640
PAGE_ORDER = ((0, 0), (0, 1), (0, 2), (1, 2), (0, 3), (1, 0), (1, 1), (1, 3))


def tile_list_zircon_peak_scores_kernel(
    tc, tab_words, tab_scales, offs, w1, gain, w2_words, w2_scales, page0, wgs, offs3,
    tab2_words, tab2_scales, offs2, pos1, pos2, terr, out,
):
    nc = tc.nc
    with ExitStack() as ctx:
        lists = ctx.enter_context(tc.tile_pool(name="lists", bufs=1))
        sb = ctx.enter_context(tc.tile_pool(name="sb", bufs=1))
        psum = ctx.enter_context(tc.psum_pool(name="psum", bufs=1))

        def new(shape, dtype, name, tag=None):
            return sb.tile(shape, dtype, name=name, tag=tag or name, align_bytes=64)

        def bank(shape, name, number):
            return psum.tile(shape, F32, name=name, tag="bank%d" % number)

        def load_list(src, name):
            tile = lists.tile([P, S // PER_COLUMN], U16, name=name)
            nc.sync.dma_start(tile[:], src)
            return tile

        def load_words(src, a, name):
            tile = new([P, T], I32, name)
            nc.sync.dma_start(out=tile[:], in_=src[a].rearrange("p t i -> p (t i)").bitcast(I32))
            return tile

        def load_w2_scales(tile):
            for quad in QUADRANT_ORDER:
                nc.scalar.dma_start(
                    out=tile[QUADRANT * quad : QUADRANT * quad + 4, :, :].bitcast(I32),
                    in_=w2_scales[:, 4 * quad : 4 * quad + 4, :].rearrange("a r c -> r a c").bitcast(I32),
                )

        def load_table_scales(tile, src):
            for quad in QUADRANT_ORDER:
                nc.gpsimd.dma_start(
                    out=tile[QUADRANT * quad : QUADRANT * quad + 4 * PASSES, :].bitcast(I32),
                    in_=src[:, 4 * quad : 4 * quad + 4, :].bitcast(I32),
                )

        def load_w1(b, a, pieces):
            rows = w1[a * KP : (a + 1) * KP, b * KP : (b + 1) * KP].rearrange("(p i) n -> p i n", i=PACK)
            width = KP // pieces
            tiles = []
            for c in range(pieces):
                tile = new([P, PACK, width], F32, "w1raw%d%d%d" % (b, a, c))
                nc.sync.dma_start(out=tile[:], in_=rows[:, :, c * width : (c + 1) * width])
                tiles.append(tile)
            return tiles

        def load_page(b, t):
            tile = new([P, T2], F32, "page%d%d" % (b, t))
            nc.sync.dma_start(out=tile[:], in_=page0.rearrange("(b p t) j -> b t p j", p=P, t=PACK)[b, t])
            return tile

        def load_wgs(t0, t1):
            tile = new([P, t1 - t0, S], F32, "wgs%d" % t0)
            rows = wgs.rearrange("(q t) j -> q t j", t=PACK)[:, t0:t1, :]
            for quad in QUADRANT_ORDER:
                nc.sync.dma_start(out=tile[QUADRANT * quad : QUADRANT * (quad + 1), :, :], in_=rows)
            return [tile[:, t - t0, :] for t in range(t0, t1)]

        def gather(dst, window, offsets):
            nc.vector.tensor_copy(dst, window.indirect(offsets))

        tab_sc = new([P, T], U8, "tab_sc")
        w2_sc_raw = new([P, PASSES, H], U8, "w2_sc_raw")
        tab2_sc = new([P, T3], U8, "tab2_sc")
        nc.vector.memset(w2_sc_raw[:].rearrange("p a c -> p (a c)").bitcast(I32), 0)
        nc.vector.memset(tab_sc[:].bitcast(I32), 0)
        nc.vector.memset(tab2_sc[:].bitcast(I32), 0)

        load_w2_scales(w2_sc_raw)
        load_table_scales(tab_sc, tab_scales)
        load_table_scales(tab2_sc, tab2_scales)
        offs_sb = load_list(offs, "offs_sb")
        offs2_sb = load_list(offs2, "offs2_sb")
        w2_raw = new([P, PASSES, H], U16, "w2_raw")
        nc.sync.dma_start(out=w2_raw[:].bitcast(I32), in_=w2_words.rearrange("a p c -> p a c").bitcast(I32))
        w1_raw = {}
        w1_raw[0, 0] = load_w1(0, 0, 1)
        w1_raw[0, 1] = load_w1(0, 1, 1)
        tab_w = [load_words(tab_words, a, "tab_w%d" % a) for a in range(PASSES)]
        gain_sb = new([P, PASSES, PACK], F32, "gain_sb")
        nc.sync.dma_start(out=gain_sb[:], in_=gain.rearrange("(b p t) -> p b t", p=P, t=PACK))
        w1_raw[1, 0] = load_w1(1, 0, 1)
        w1_raw[1, 1] = load_w1(1, 1, 2)
        offs3_sb = load_list(offs3, "offs3_sb")
        page = {}
        page[0, 0] = load_page(0, 0)
        wgs_sb = load_wgs(0, 1)
        tab2_w = [load_words(tab2_words, 0, "tab2_w0")]
        page[0, 1] = load_page(0, 1)
        wgs_sb.extend(load_wgs(1, 2))
        page[0, 2] = load_page(0, 2)
        wgs_sb.extend(load_wgs(2, PACK))
        page[1, 2] = load_page(1, 2)
        page[0, 3] = load_page(0, 3)
        tab2_w.append(load_words(tab2_words, 1, "tab2_w1"))
        for t in (0, 1, 3):
            page[1, t] = load_page(1, t)
        pos1_sb = load_list(pos1, "pos1_sb")
        pos2_sb = load_list(pos2, "pos2_sb")
        terr_sb = new([P, S2 // P], F32, "terr_sb")
        with nc.allow_non_contiguous_dma(reason="terr[128 u + p] goes to partition p, column u"):
            nc.sync.dma_start(out=terr_sb[:], in_=terr.rearrange("(u p) -> p u", p=P))

        w1_codes, w1_sc = {}, {}

        def weave_w1(engine_copy, dst, raw, q0, q1):
            engine_copy(
                out=dst[:, :, q0:q1, :].rearrange("p t q i -> p q i t"),
                in_=raw[:].rearrange("p i (q t) -> p q i t", t=PACK),
            )

        def quantize_w1(b, a, woven_tile):
            w1_codes[b, a] = new([P, KP], U32, "w1c%d%d" % (b, a))
            w1_sc[b, a] = new([P, KP], U8, "w1s%d%d" % (b, a))
            nc.vector.quantize_mx(
                out=w1_codes[b, a][:].bitcast(FP8X4), scales=w1_sc[b, a][:],
                in_=woven_tile[:].rearrange("p t q i -> p (t q i)"),
            )

        w1_bf = {}
        for a in range(PASSES):
            w1_bf[0, a] = new([P, PACK, P, PACK], BF16, "w1bf0%d" % a, tag="w1bf%d" % a)
        weave_w1(nc.scalar.copy, w1_bf[0, 0], w1_raw[0, 0][0], 0, P)
        weave_w1(nc.scalar.copy, w1_bf[0, 1], w1_raw[0, 1][0], 0, P)

        w2_codes = new([P, PASSES, H], U16, "w2_c")
        nc.vector.tensor_copy(
            out=w2_codes[:].rearrange("p a (b t q) -> p (a b) t q", t=PACK, q=P),
            in_=w2_raw[:].rearrange("p a (b q t) -> p (a b) t q", t=PACK, q=P),
        )
        w2_sc = new([P, PASSES, H], U8, "w2_sc")
        nc.vector.tensor_copy(
            out=w2_sc[:].rearrange("p a (b t q) -> p (a b) t q", t=PACK, q=P),
            in_=w2_sc_raw[:].rearrange("p a (b q t) -> p (a b) t q", t=PACK, q=P),
        )
        v_sc = new([P, S], U8, "v_sc")
        gather(v_sc[:], tab_sc[:], offs_sb[:])
        quantize_w1(0, 0, w1_bf[0, 0])
        v_codes = []
        for a in range(PASSES):
            v_codes.append(new([P, S], U32, "v%d" % a))
            gather(v_codes[a][:], tab_w[a][:].bitcast(U32), offs_sb[:])
        quantize_w1(0, 1, w1_bf[0, 1])

        for a in range(PASSES):
            w1_bf[1, a] = new([P, PACK, P, PACK], BF16, "w1bf1%d" % a, tag="w1bf%d" % a)
        weave_w1(nc.vector.tensor_copy, w1_bf[1, 0], w1_raw[1, 0][0], 0, P)
        quantize_w1(1, 0, w1_bf[1, 0])
        weave_w1(nc.scalar.copy, w1_bf[1, 1], w1_raw[1, 1][0], 0, P // 2)
        weave_w1(nc.vector.tensor_copy, w1_bf[1, 1], w1_raw[1, 1][1], P // 2, P)
        quantize_w1(1, 1, w1_bf[1, 1])

        v2_sc = new([P, S2], U8, "v2_sc", tag="tab_w1")
        gather(v2_sc[:], tab2_sc[:], offs2_sb[:])

        x_codes, x_sc = [], []
        for b in range(PASSES):
            acc = [bank([P, PACK, JQ], "acc1_%d%d" % (b, jq), PACK * b + jq) for jq in range(S // JQ)]
            for jq in range(S // JQ):
                for a in range(PASSES):
                    cols = slice(jq * JQ, (jq + 1) * JQ)
                    for t in range(PACK):
                        nc.tensor.matmul_mx(
                            out=acc[jq][:, t, :],
                            lhsT=w1_codes[b, a][:, t * P : (t + 1) * P].bitcast(FP8X4),
                            lhsT_scale=w1_sc[b, a][:, t * P : (t + 1) * P],
                            rhs=v_codes[a][:, cols].bitcast(FP8X4),
                            rhs_scale=v_sc[4 * a : P, cols],
                            start=(a == 0 and t == 0),
                            stop=(a == PASSES - 1 and t == PACK - 1),
                        )
            x_bf = new([P, S, PACK], BF16, "x_bf%d" % b, tag=("w1bf0", "x_bf1")[b])
            x_codes.append(new([P, S], U32, "x_c%d" % b, tag=("w1bf1", "x_c1")[b]))
            x_sc.append(new([P, S], U8, "x_s%d" % b))
            for jq in range(S // JQ):
                th = new([P, JQ, PACK], F32, "th%d%d" % (b, jq))
                nc.scalar.activation(out=th[:], in_=acc[jq][:].rearrange("p t j -> p j t"), func=TANH)
                nc.vector.tensor_tensor(
                    out=x_bf[:, jq * JQ : (jq + 1) * JQ, :], in0=th[:],
                    in1=gain_sb[:, b : b + 1, :].to_broadcast([P, JQ, PACK]), op=ALU.mult,
                )
            for half in range(2):
                cols = slice(half * S // 2, (half + 1) * S // 2)
                nc.vector.quantize_mx(
                    out=x_codes[b][:, cols].bitcast(FP8X4), scales=x_sc[b][:, cols],
                    in_=x_bf[:, cols, :].rearrange("p j t -> p (j t)"),
                )

        v2_codes = {}
        v2_codes[0, 0] = new([P, S2], U32, "v2_0", tag="x_bf1")
        v2_codes[0, 1] = v2_codes[0, 0][:, S2 // 2 : S2]
        gather(v2_codes[0, 0][:], tab2_w[0][:].bitcast(U32), offs2_sb[:])
        half_list = S2 // 2 // PER_COLUMN

        h = {}
        for n, (b, t) in enumerate(PAGE_ORDER):
            tile_number = PACK * b + t
            cols = slice(tile_number * P, (tile_number + 1) * P)
            acc2 = bank([P, S], "acc2_%d" % tile_number, n)
            for a in range(PASSES):
                nc.tensor.matmul_mx(
                    out=acc2[:],
                    lhsT=w2_codes[:, a, cols].bitcast(FP4X4),
                    lhsT_scale=w2_sc[:, a, cols],
                    rhs=x_codes[a][:].bitcast(FP8X4),
                    rhs_scale=x_sc[a][:],
                    start=(a == 0),
                    stop=(a == PASSES - 1),
                )
            h[b, t] = new([P, S], F32, "h%d" % tile_number)
            nc.scalar.copy(out=h[b, t][:], in_=acc2[:])

        page_bf = [new([P, T2, PACK], BF16, "page_bf%d" % b) for b in range(PASSES)]
        page_sc = [new([P, T2], U8, "page_s%d" % b) for b in range(PASSES)]
        page_codes = []
        last = len(PAGE_ORDER) - 1
        for n, (b, t) in enumerate(PAGE_ORDER):
            nc.vector.tensor_tensor(page[b, t][:].indirect(offs3_sb[:]), h[b, t][:], wgs_sb[t], ALU.mult)
            if n < last:
                nc.scalar.copy(out=page_bf[b][:, :, t], in_=page[b, t][:])
            if n == last // 2:
                v2_codes[1, 0] = new([P, S2 // 2], U32, "v2_10")
                gather(v2_codes[1, 0][:], tab2_w[1][:].bitcast(U32), offs2_sb[:, 0:half_list])
            if n == last - 1:
                page_codes.append(new([P, T2], U32, "page_c0", tag="h%d" % (PACK * b + t)))
                nc.vector.quantize_mx(
                    out=page_codes[0][:].bitcast(FP8X4), scales=page_sc[0][:],
                    in_=page_bf[0][:].rearrange("p j t -> p (j t)"),
                )
        b, t = PAGE_ORDER[last]
        nc.vector.tensor_copy(out=page_bf[b][:, 0:BANK, t], in_=page[b, t][:, 0:BANK])
        nc.vector.tensor_copy(out=page_bf[b][:, BANK:VECTOR_COLUMNS, t], in_=page[b, t][:, BANK:VECTOR_COLUMNS])
        nc.scalar.copy(out=page_bf[b][:, VECTOR_COLUMNS:T2, t], in_=page[b, t][:, VECTOR_COLUMNS:T2])
        page_codes.append(new([P, T2], U32, "page_c1"))
        for half in range(T2 // BANK):
            cols = slice(half * BANK, (half + 1) * BANK)
            nc.vector.quantize_mx(
                out=page_codes[b][:, cols].bitcast(FP8X4), scales=page_sc[b][:, cols],
                in_=page_bf[b][:, cols, :].rearrange("p j t -> p (j t)"),
            )
        v2_codes[1, 1] = new([P, S2 // 2], U32, "v2_11", tag="page_bf1")
        gather(v2_codes[1, 1][:], tab2_w[1][:].bitcast(U32), offs2_sb[:, half_list : 2 * half_list])

        tiles = S2 // P
        acc3 = [[bank([P, BANK], "acc3_%d%d" % (u, half), 2 * u + half) for half in range(2)] for u in range(tiles)]
        for a in range(PASSES):
            for u in range(tiles):
                for half in range(2):
                    cols = slice(half * BANK, (half + 1) * BANK)
                    nc.tensor.matmul_mx(
                        out=acc3[u][half][:],
                        lhsT=v2_codes[a, u // 2][:, (u % 2) * P : (u % 2 + 1) * P].bitcast(FP8X4),
                        lhsT_scale=v2_sc[4 * a : P, u * P : (u + 1) * P],
                        rhs=page_codes[a][:, cols].bitcast(FP8X4),
                        rhs_scale=page_sc[a][:, cols],
                        start=(a == 0),
                        stop=(a == PASSES - 1),
                    )
        e = []
        for u in range(tiles):
            e.append(new([P, T2], F32, "e%d" % u, tag="w1raw%d%d0" % (u // 2, u % 2)))
            for half in range(2):
                copy = nc.vector.tensor_copy if (u, half) == (0, 1) else nc.scalar.copy
                copy(out=e[u][:, half * BANK : (half + 1) * BANK], in_=acc3[u][half][:])

        steps = [(u, 0, NPAIR) for u in range(tiles - 1)] + [(tiles - 1, 0, NPAIR // 2), (tiles - 1, NPAIR // 2, NPAIR)]
        picked = []

        def finish(n):
            u, j0, j1 = steps[n]
            core, rim = picked[n]
            res = new([P, j1 - j0], F32, "res%d" % n, tag="th0%d" % (n % PACK))
            nc.vector.scalar_tensor_tensor(
                out=res[:], in0=rim[:], scalar=terr_sb[:, u : u + 1], in1=core[:], op0=ALU.add, op1=ALU.max
            )
            nc.sync.dma_start(out=out[u * P : (u + 1) * P, j0:j1], in_=res[:])

        for n, (u, j0, j1) in enumerate(steps):
            entries = slice(j0 // PER_COLUMN, j1 // PER_COLUMN)
            core = new([P, j1 - j0], F32, "core%d" % n, tag="th1%d" % (n % PACK))
            rim = new([P, j1 - j0], F32, "rim%d" % n, tag="h%d" % n)
            picked.append((core, rim))
            gather(core[:], e[u][:], pos1_sb[:, entries])
            if n > 0:
                finish(n - 1)
            gather(rim[:], e[u][:], pos2_sb[:, entries])
        finish(len(steps) - 1)
